import numpy as np
import ml_dtypes


def mxq(x, axis, fmt="e4m3"):
    dtype, down = {"e4m3": (ml_dtypes.float8_e4m3fn, 7), "e5m2": (ml_dtypes.float8_e5m2, 14)}[fmt]
    v = np.moveaxis(np.asarray(x, np.float32).astype(ml_dtypes.bfloat16).astype(np.float64), axis, -1)
    blocks = v.reshape(v.shape[:-1] + (-1, 32))
    amax = np.abs(blocks).max(-1, keepdims=True)
    byte = np.maximum(np.where(amax > 0, np.frexp(amax)[1] - 1 + 127, 0) - down, 1)
    scale = np.exp2(byte - 127.0)
    codes = (blocks / scale).astype(np.float32).astype(dtype).astype(np.float64)
    return np.moveaxis((codes * scale).reshape(v.shape), -1, axis)


WIDE = False


def mx_kscale(k):
    if not WIDE:
        return np.ones(k)
    levels = np.array([10, -10, 5, -5, 0])
    if k % 512:
        return np.exp2(np.random.permutation(np.resize(levels, k // 32))).repeat(32)
    a = np.empty((k // 512, 16))
    for p in range(k // 512):
        a[p, :8] = np.random.permutation(np.resize(levels, 8))
        for g in range(8):
            far = levels[np.abs(levels - a[p, g]) >= 10]
            a[p, g + 8] = far[np.random.randint(len(far))]
    return np.exp2(a.ravel()).repeat(32)


def f64(x):
    return np.asarray(x).astype(np.float64)


def striped(idx):
    return np.tile(np.asarray(idx).reshape(-1, 16).T, (8, 1)).astype(np.uint16)


def unstriped(offs):
    return offs[:16].T.reshape(-1).astype(np.int64)


def striped8(idx):
    return np.asarray(idx).reshape(8, -1, 16).transpose(0, 2, 1).reshape(128, -1).astype(np.uint16)


def unstriped8(offs):
    return offs.reshape(8, 16, -1).transpose(0, 2, 1).reshape(8, -1).astype(np.int64)


def pick8(x, idx, run):
    r = np.arange(len(x))
    return x[r[:, None], idx[r % (8 * run) // run]]


E2M1 = np.array([0.0, 0.5, 1.0, 1.5, 2.0, 3.0, 4.0, 6.0, -0.0, -0.5, -1.0, -1.5, -2.0, -3.0, -4.0, -6.0])


def pack_weight(w, fmt):
    k, n = w.shape
    w = f64(np.asarray(w, np.float32).astype(ml_dtypes.bfloat16)).reshape(k // 32, 32, n)
    amax = np.abs(w).max(1)
    if fmt == "e4m3":
        byte = np.frexp(amax)[1] - 1 + 127 - 7
    else:
        mant, ex = np.frexp(amax / 6.0)
        byte = np.where(mant > 0.5, ex, ex - 1) + 127
    byte = np.clip(np.where(amax > 0, byte, 1), 1, 254)
    scaled = (w * np.exp2(127.0 - byte)[:, None, :]).reshape(k, n).astype(np.float32)
    by_word = np.ascontiguousarray(scaled.reshape(k // 512, 128, 4, n).transpose(0, 1, 3, 2))
    if fmt == "e4m3":
        words = by_word.astype(ml_dtypes.float8_e4m3fn).view(np.uint8)
    else:
        c = by_word.astype(ml_dtypes.float4_e2m1fn).view(np.uint8) & 0xF
        words = (c[..., 0::2] | (c[..., 1::2] << 4)).reshape(k // 512, 128, 2 * n)
    return np.ascontiguousarray(words), np.ascontiguousarray(byte.astype(np.uint8).reshape(k // 512, 16, n))


def unpack_weight(words, scales, fmt):
    g, _, n = scales.shape
    words = np.ascontiguousarray(words).reshape(g, 128, n, -1)
    if fmt == "e4m3":
        vals = words.view(ml_dtypes.float8_e4m3fn).astype(np.float64)
    else:
        nib = np.empty((g, 128, n, 4), np.uint8)
        nib[..., 0::2] = words & 0xF
        nib[..., 1::2] = words >> 4
        vals = E2M1[nib]
    vals = vals * np.repeat(np.exp2(scales.astype(np.float64) - 127.0), 8, axis=1)[..., None]
    return vals.transpose(0, 1, 3, 2).reshape(g * 512, n)


K, T, J, R, N, V = 512, 1024, 512, 512, 512, 512


def setup_inputs():
    n = np.random.standard_normal
    idx = np.random.permutation(T)[:J]
    idx2 = np.stack([np.random.randint(0, V, J) for _ in range(8)])
    fk = mx_kscale(K)
    fr = mx_kscale(R)
    xtp = pack_weight(n((K, T)) / fk[:, None], "e4m3")
    wap = pack_weight(n((K, R)) * 1 / np.sqrt(K) * fk[:, None] * fr, "e2m1")
    wbp = pack_weight(n((R, N)) * 1 / np.sqrt(R) / fr[:, None], "e4m3")
    return {
        "xt_words": xtp[0],
        "xt_scales": xtp[1],
        "wa_words": wap[0],
        "wa_scales": wap[1],
        "tb": (n((R, V)) * 0.7 * fr[:, None]).astype(np.float32),
        "wb_words": wbp[0],
        "wb_scales": wbp[1],
        "offs": striped(idx),
        "offs2": striped8(idx2),
    }


def reference(xt_words, xt_scales, wa_words, wa_scales, tb, wb_words, wb_scales, offs, offs2):
    idx = unstriped(offs)
    idx2 = unstriped8(offs2)
    xtu = unpack_weight(xt_words, xt_scales, "e4m3")
    wau = unpack_weight(wa_words, wa_scales, "e2m1")
    wbu = unpack_weight(wb_words, wb_scales, "e4m3")
    xtidxg = xtu[:, idx]
    a = wau.T @ xtidxg
    hid = np.maximum(a, 0.0) + pick8(f64(tb), idx2, 64)
    hidq = mxq(hid, 0, "e4m3")
    y = wbu.T @ hidq
    return y

@@ -1,0 +1,163 @@
+from contextlib import ExitStack
+
+import concourse.mybir as mybir
+
+K, T, J, R, N, V = 512, 1024, 512, 512, 512, 512
+FLOPS = 2 * K * R * J + 2 * R * N * J
+
+F32 = mybir.dt.float32
+BF16 = mybir.dt.bfloat16
+I32 = mybir.dt.int32
+U32 = mybir.dt.uint32
+U16 = mybir.dt.uint16
+U8 = mybir.dt.uint8
+FP8X4 = mybir.dt.float8_e4m3fn_x4
+FP4X4 = mybir.dt.float4_e2m1fn_x4
+ADD = mybir.AluOpType.add
+RELU = mybir.ActivationFunctionType.Relu
+
+P = 128
+PACK = 4
+HALF = 256
+CHUNK = 128
+
+
+def load_scale_rows(queue, plane, scales):
+    for r in range(4):
+        queue.dma_start(out=plane[r:P:32, :].bitcast(I32), in_=scales[0, r:16:4, :].bitcast(I32))
+
+
+def tile_moe_expert_hidden_own_entries_kernel(
+    tc, xt_words, xt_scales, wa_words, wa_scales, tb, wb_words, wb_scales, offs, offs2, out
+):
+    nc = tc.nc
+    with ExitStack() as ctx:
+        held = ctx.enter_context(tc.tile_pool(name="held", bufs=1))
+        psum = ctx.enter_context(tc.psum_pool(name="psum", bufs=1))
+
+        tok_list = held.tile([P, J // 16], U16, name="tok_list")
+        ent_lists = held.tile([P, J // 16], U16, name="ent_lists")
+        x_words = held.tile([P, T], U32, name="x_words", align_bytes=64)
+        x_plane = held.tile([P, T], U8, name="x_plane", align_bytes=64)
+        wa_raw = held.tile([P, 2 * R], U8, name="wa_raw", align_bytes=64)
+        wa_raw_plane = held.tile([P, R], U8, name="wa_raw_plane", tag="early", align_bytes=64)
+        wa = held.tile([P, 2 * R], U8, name="wa", align_bytes=64)
+        wa_plane = held.tile([P, R], U8, name="wa_plane", align_bytes=64)
+        wb = held.tile([P, N], U32, name="wb", align_bytes=64)
+        wb_plane = held.tile([P, N], U8, name="wb_plane", align_bytes=64)
+        table = [held.tile([P, V], F32, name="table%d" % t, align_bytes=64) for t in range(PACK)]
+        xg_plane = held.tile([P, J], U8, name="xg_plane", align_bytes=64)
+        relu = [held.tile([P, J], F32, name="relu%d" % t, align_bytes=64) for t in range(PACK)]
+
+        nc.vector.memset(x_plane[:].bitcast(I32), 0)
+        nc.gpsimd.memset(wa_raw_plane[:].bitcast(I32), 0)
+        nc.vector.memset(wb_plane[:].bitcast(I32), 0)
+        nc.sync.dma_start(tok_list[:], offs)
+        nc.sync.dma_start(out=wa_raw[:].bitcast(I32), in_=wa_words[0].bitcast(I32))
+        load_scale_rows(nc.sync, x_plane, xt_scales)
+        nc.sync.dma_start(out=x_words[:].bitcast(I32), in_=xt_words[0].rearrange("p t r -> p (t r)").bitcast(I32))
+        load_scale_rows(nc.sync, wa_raw_plane, wa_scales)
+        nc.sync.dma_start(ent_lists[:], offs2)
+        tb_rows = tb.rearrange("(p t) v -> p t v", t=PACK)
+        for t in range(PACK):
+            nc.sync.dma_start(out=table[t][:], in_=tb_rows[:, t, :])
+        nc.sync.dma_start(out=wb[:].bitcast(I32), in_=wb_words[0].rearrange("p n r -> p (n r)").bitcast(I32))
+        load_scale_rows(nc.sync, wb_plane, wb_scales)
+
+        nc.vector.tensor_copy(
+            out=wa_plane[:].rearrange("p (t m) -> p t m", t=PACK),
+            in_=wa_raw_plane[:].rearrange("p (m t) -> p t m", t=PACK),
+        )
+        nc.vector.tensor_copy(
+            out=wa[:].bitcast(U16).rearrange("p (t m) -> p t m", t=PACK),
+            in_=wa_raw[:].bitcast(U16).rearrange("p (m t) -> p t m", t=PACK),
+        )
+
+        pre = [psum.tile([P, J], F32, name="pre%d" % t, tag="pre%d" % t) for t in range(PACK)]
+        for j0 in range(0, J, HALF):
+            slots = slice(j0, j0 + HALF)
+            entries = tok_list[:, j0 // 16 : (j0 + HALF) // 16]
+            xg_words = held.tile([P, HALF], U32, name="xg_words", tag="early" if j0 else "xg_first", align_bytes=64)
+            nc.vector.tensor_copy(out=xg_plane[:, slots], in_=x_plane[:].indirect(entries))
+            nc.vector.tensor_copy(out=xg_words[:], in_=x_words[:].indirect(entries))
+            for t in range(PACK):
+                nc.tensor.matmul_mx(
+                    out=pre[t][:, slots],
+                    lhsT=wa[:, 2 * P * t : 2 * P * (t + 1)].bitcast(FP4X4),
+                    lhsT_scale=wa_plane[:, P * t : P * (t + 1)],
+                    rhs=xg_words[:].bitcast(FP8X4),
+                    rhs_scale=xg_plane[:, slots],
+                    start=True,
+                    stop=True,
+                )
+                nc.scalar.activation(out=relu[t][:, slots], in_=pre[t][:, slots], func=RELU)
+
+        out_rows = out.rearrange("(b p) j -> p b j", p=P)
+        chunks = J // CHUNK
+        last = chunks - 1
+        hid, woven, acc = {}, {}, {}
+
+        def add_entries(c):
+            slots = slice(c * CHUNK, (c + 1) * CHUNK)
+            entries = ent_lists[:, c * CHUNK // 16 : (c + 1) * CHUNK // 16]
+            hid[c] = held.tile([P, PACK, CHUNK], F32, name="hid", tag="stage%d" % c, align_bytes=64)
+            for t in range(PACK):
+                nc.vector.tensor_tensor(out=hid[c][:, t, :], in0=table[t][:].indirect(entries), in1=relu[t][:, slots], op=ADD)
+
+        def weave(c):
+            woven[c] = held.tile([P, CHUNK * PACK], BF16, name="woven", tag="stage%d" % (c + 2), align_bytes=64)
+            dst = woven[c][:].rearrange("p (g i t) -> p g t i", i=4, t=PACK)
+            src = hid[c][:].rearrange("p t (g i) -> p g t i", i=4)
+            if c == last:
+                nc.vector.tensor_copy(out=dst, in_=src)
+            else:
+                nc.scalar.copy(out=dst, in_=src)
+
+        def second_layer(c):
+            h_words = held.tile([P, CHUNK], U32, name="h_words", tag="h_words%d" % c, align_bytes=64)
+            h_plane = held.tile([P, CHUNK], U8, name="h_plane", tag="h_plane%d" % c, align_bytes=64)
+            nc.vector.quantize_mx(out=h_words[:].bitcast(FP8X4), scales=h_plane[:], in_=woven[c][:])
+            parts = 2 if c == last else 1
+            blocks = N // P // parts
+            acc[c] = []
+            for part in range(parts):
+                bank = psum.tile([P, blocks, CHUNK], F32, name="acc", tag="pre0" if part else "acc%d" % c)
+                acc[c].append(bank)
+                for b in range(blocks):
+                    cols = slice(P * (part * blocks + b), P * (part * blocks + b + 1))
+                    nc.tensor.matmul_mx(
+                        out=bank[:, b, :],
+                        lhsT=wb[:, cols].bitcast(FP8X4),
+                        lhsT_scale=wb_plane[:, cols],
+                        rhs=h_words[:].bitcast(FP8X4),
+                        rhs_scale=h_plane[:],
+                        start=True,
+                        stop=True,
+                    )
+
+        def store(c):
+            slots = slice(c * CHUNK, (c + 1) * CHUNK)
+            parts = len(acc[c])
+            blocks = N // P // parts
+            for part in range(parts):
+                res = held.tile([P, blocks, CHUNK], F32, name="res", tag="res%d_%d" % (c, part), align_bytes=64)
+                rows = out_rows[:, part * blocks : (part + 1) * blocks, slots]
+                if c == last and part == 0:
+                    nc.vector.tensor_copy(out=res[:], in_=acc[c][part][:])
+                    nc.sync.dma_start(out=rows, in_=res[:])
+                elif c == last:
+                    nc.scalar.copy(out=res[:], in_=acc[c][part][:])
+                    nc.scalar.dma_start(out=rows, in_=res[:])
+                else:
+                    nc.scalar.copy(out=res[:], in_=acc[c][part][:])
+                    nc.sync.dma_start(out=rows, in_=res[:])
+
+        for c in range(chunks):
+            add_entries(c)
+            if c > 0:
+                second_layer(c - 1)
+            weave(c)
+            if c > 0:
+                store(c - 1)
+        second_layer(last)
+        store(last)

@@ -18,146 +18,151 @@ RELU = mybir.ActivationFunctionType.Relu
 
 P = 128
 PACK = 4
-HALF = 256
+GROUP = 16
+QUADRANT = 32
 CHUNK = 128
+HALF = J // 2
+ALIGN = 64
 
 
-def load_scale_rows(queue, plane, scales):
-    for r in range(4):
-        queue.dma_start(out=plane[r:P:32, :].bitcast(I32), in_=scales[0, r:16:4, :].bitcast(I32))
+def load_scale_rows(nc, plane, scales):
+    for i in range(4):
+        nc.sync.dma_start(out=plane[i:P:QUADRANT, :].bitcast(I32), in_=scales[0, i:16:4, :].bitcast(I32))
+
+
+def by_sheet(raw):
+    return raw.rearrange("p (m t) -> p t m", t=PACK)
 
 
 def tile_moe_expert_hidden_own_entries_kernel(
     tc, xt_words, xt_scales, wa_words, wa_scales, tb, wb_words, wb_scales, offs, offs2, out
 ):
     nc = tc.nc
+    chunks = J // CHUNK
+    last = chunks - 1
     with ExitStack() as ctx:
-        held = ctx.enter_context(tc.tile_pool(name="held", bufs=1))
+        sbuf = ctx.enter_context(tc.tile_pool(name="sbuf", bufs=1))
         psum = ctx.enter_context(tc.psum_pool(name="psum", bufs=1))
 
-        tok_list = held.tile([P, J // 16], U16, name="tok_list")
-        ent_lists = held.tile([P, J // 16], U16, name="ent_lists")
-        x_words = held.tile([P, T], U32, name="x_words", align_bytes=64)
-        x_plane = held.tile([P, T], U8, name="x_plane", align_bytes=64)
-        wa_raw = held.tile([P, 2 * R], U8, name="wa_raw", align_bytes=64)
-        wa_raw_plane = held.tile([P, R], U8, name="wa_raw_plane", tag="early", align_bytes=64)
-        wa = held.tile([P, 2 * R], U8, name="wa", align_bytes=64)
-        wa_plane = held.tile([P, R], U8, name="wa_plane", align_bytes=64)
-        wb = held.tile([P, N], U32, name="wb", align_bytes=64)
-        wb_plane = held.tile([P, N], U8, name="wb_plane", align_bytes=64)
-        table = [held.tile([P, V], F32, name="table%d" % t, align_bytes=64) for t in range(PACK)]
-        xg_plane = held.tile([P, J], U8, name="xg_plane", align_bytes=64)
-        relu = [held.tile([P, J], F32, name="relu%d" % t, align_bytes=64) for t in range(PACK)]
+        token_list = sbuf.tile([P, J // GROUP], U16, name="token_list")
+        entry_lists = sbuf.tile([P, J // GROUP], U16, name="entry_lists")
+        x_words = sbuf.tile([P, T], U32, name="x_words", align_bytes=ALIGN)
+        x_plane = sbuf.tile([P, T], U8, name="x_plane", align_bytes=ALIGN)
+        wa_raw = sbuf.tile([P, 2 * R], U8, name="wa_raw", align_bytes=ALIGN)
+        wa_raw_plane = sbuf.tile([P, R], U8, name="wa_raw_plane", tag="early", align_bytes=ALIGN)
+        wa = sbuf.tile([P, 2 * R], U8, name="wa", align_bytes=ALIGN)
+        wa_plane = sbuf.tile([P, R], U8, name="wa_plane", align_bytes=ALIGN)
+        wb = sbuf.tile([P, N], U32, name="wb", align_bytes=ALIGN)
+        wb_plane = sbuf.tile([P, N], U8, name="wb_plane", align_bytes=ALIGN)
+        table = [sbuf.tile([P, V], F32, name="table%d" % t, align_bytes=ALIGN) for t in range(PACK)]
+        xg_plane = sbuf.tile([P, J], U8, name="xg_plane", align_bytes=ALIGN)
 
         nc.vector.memset(x_plane[:].bitcast(I32), 0)
         nc.gpsimd.memset(wa_raw_plane[:].bitcast(I32), 0)
         nc.vector.memset(wb_plane[:].bitcast(I32), 0)
-        nc.sync.dma_start(tok_list[:], offs)
+
+        nc.sync.dma_start(token_list[:], offs)
+        nc.sync.dma_start(entry_lists[:], offs2)
         nc.sync.dma_start(out=wa_raw[:].bitcast(I32), in_=wa_words[0].bitcast(I32))
-        load_scale_rows(nc.sync, x_plane, xt_scales)
+        load_scale_rows(nc, x_plane, xt_scales)
         nc.sync.dma_start(out=x_words[:].bitcast(I32), in_=xt_words[0].rearrange("p t r -> p (t r)").bitcast(I32))
-        load_scale_rows(nc.sync, wa_raw_plane, wa_scales)
-        nc.sync.dma_start(ent_lists[:], offs2)
-        tb_rows = tb.rearrange("(p t) v -> p t v", t=PACK)
+        load_scale_rows(nc, wa_raw_plane, wa_scales)
+        tb_sheets = tb.rearrange("(p t) v -> p t v", t=PACK)
         for t in range(PACK):
-            nc.sync.dma_start(out=table[t][:], in_=tb_rows[:, t, :])
+            nc.sync.dma_start(out=table[t][:], in_=tb_sheets[:, t, :])
         nc.sync.dma_start(out=wb[:].bitcast(I32), in_=wb_words[0].rearrange("p n r -> p (n r)").bitcast(I32))
-        load_scale_rows(nc.sync, wb_plane, wb_scales)
+        load_scale_rows(nc, wb_plane, wb_scales)
 
+        nc.vector.tensor_copy(out=wa_plane[:].rearrange("p (t m) -> p t m", t=PACK), in_=by_sheet(wa_raw_plane[:]))
         nc.vector.tensor_copy(
-            out=wa_plane[:].rearrange("p (t m) -> p t m", t=PACK),
-            in_=wa_raw_plane[:].rearrange("p (m t) -> p t m", t=PACK),
-        )
-        nc.vector.tensor_copy(
-            out=wa[:].bitcast(U16).rearrange("p (t m) -> p t m", t=PACK),
-            in_=wa_raw[:].bitcast(U16).rearrange("p (m t) -> p t m", t=PACK),
+            out=wa[:].bitcast(U16).rearrange("p (t m) -> p t m", t=PACK), in_=by_sheet(wa_raw[:].bitcast(U16))
         )
 
-        pre = [psum.tile([P, J], F32, name="pre%d" % t, tag="pre%d" % t) for t in range(PACK)]
-        for j0 in range(0, J, HALF):
-            slots = slice(j0, j0 + HALF)
-            entries = tok_list[:, j0 // 16 : (j0 + HALF) // 16]
-            xg_words = held.tile([P, HALF], U32, name="xg_words", tag="early" if j0 else "xg_first", align_bytes=64)
-            nc.vector.tensor_copy(out=xg_plane[:, slots], in_=x_plane[:].indirect(entries))
-            nc.vector.tensor_copy(out=xg_words[:], in_=x_words[:].indirect(entries))
-            for t in range(PACK):
-                nc.tensor.matmul_mx(
-                    out=pre[t][:, slots],
-                    lhsT=wa[:, 2 * P * t : 2 * P * (t + 1)].bitcast(FP4X4),
-                    lhsT_scale=wa_plane[:, P * t : P * (t + 1)],
-                    rhs=xg_words[:].bitcast(FP8X4),
-                    rhs_scale=xg_plane[:, slots],
-                    start=True,
-                    stop=True,
-                )
-                nc.scalar.activation(out=relu[t][:, slots], in_=pre[t][:, slots], func=RELU)
+        nc.vector.tensor_copy(out=xg_plane[:], in_=x_plane[:].indirect(token_list[:]))
+        xg_words = []
+        for h, tag in enumerate(("xg_first", "early")):
+            gathered = sbuf.tile([P, HALF], U32, name="xg_words", tag=tag, align_bytes=ALIGN)
+            entries = token_list[:, h * HALF // GROUP : (h + 1) * HALF // GROUP]
+            nc.vector.tensor_copy(out=gathered[:], in_=x_words[:].indirect(entries))
+            xg_words.append(gathered)
 
-        out_rows = out.rearrange("(b p) j -> p b j", p=P)
-        chunks = J // CHUNK
-        last = chunks - 1
-        hid, woven, acc = {}, {}, {}
+        relu, woven, sums = {}, {}, {}
+
+        def first_layer(c, banks):
+            j0 = c * CHUNK
+            sheets = PACK // len(banks)
+            relu[c] = sbuf.tile([P, PACK, CHUNK], F32, name="relu", tag="relu%d" % c if c else "stage1", align_bytes=ALIGN)
+            for part, bank in enumerate(banks):
+                pre = psum.tile([P, sheets, CHUNK], F32, name="pre", tag="bank%d" % bank)
+                for s in range(sheets):
+                    t = part * sheets + s
+                    nc.tensor.matmul_mx(
+                        out=pre[:, s, :],
+                        lhsT=wa[:, 2 * P * t : 2 * P * (t + 1)].bitcast(FP4X4),
+                        lhsT_scale=wa_plane[:, P * t : P * (t + 1)],
+                        rhs=xg_words[j0 // HALF][:, j0 % HALF : j0 % HALF + CHUNK].bitcast(FP8X4),
+                        rhs_scale=xg_plane[:, j0 : j0 + CHUNK],
+                        start=True,
+                        stop=True,
+                    )
+                nc.scalar.activation(out=relu[c][:, part * sheets : (part + 1) * sheets, :], in_=pre[:], func=RELU)
 
         def add_entries(c):
-            slots = slice(c * CHUNK, (c + 1) * CHUNK)
-            entries = ent_lists[:, c * CHUNK // 16 : (c + 1) * CHUNK // 16]
-            hid[c] = held.tile([P, PACK, CHUNK], F32, name="hid", tag="stage%d" % c, align_bytes=64)
+            entries = entry_lists[:, c * CHUNK // GROUP : (c + 1) * CHUNK // GROUP]
+            hid = sbuf.tile([P, PACK, CHUNK], F32, name="hid", tag="stage%d" % c, align_bytes=ALIGN)
             for t in range(PACK):
-                nc.vector.tensor_tensor(out=hid[c][:, t, :], in0=table[t][:].indirect(entries), in1=relu[t][:, slots], op=ADD)
+                nc.vector.tensor_tensor(out=hid[:, t, :], in0=table[t][:].indirect(entries), in1=relu[c][:, t, :], op=ADD)
+            return hid
 
-        def weave(c):
-            woven[c] = held.tile([P, CHUNK * PACK], BF16, name="woven", tag="stage%d" % (c + 2), align_bytes=64)
-            dst = woven[c][:].rearrange("p (g i t) -> p g t i", i=4, t=PACK)
-            src = hid[c][:].rearrange("p t (g i) -> p g t i", i=4)
-            if c == last:
-                nc.vector.tensor_copy(out=dst, in_=src)
-            else:
-                nc.scalar.copy(out=dst, in_=src)
+        def weave(copy, c, hid):
+            woven[c] = sbuf.tile([P, CHUNK * PACK], BF16, name="woven", tag="stage%d" % (c + 2), align_bytes=ALIGN)
+            copy(
+                out=woven[c][:].rearrange("p (g i t) -> p g t i", i=2, t=PACK),
+                in_=hid[:].rearrange("p t (g i) -> p g t i", i=2),
+            )
 
-        def second_layer(c):
-            h_words = held.tile([P, CHUNK], U32, name="h_words", tag="h_words%d" % c, align_bytes=64)
-            h_plane = held.tile([P, CHUNK], U8, name="h_plane", tag="h_plane%d" % c, align_bytes=64)
+        def second_layer(c, banks):
+            h_words = sbuf.tile([P, CHUNK], U32, name="h_words", tag="h_words%d" % c, align_bytes=ALIGN)
+            h_plane = sbuf.tile([P, CHUNK], U8, name="h_plane", tag="h_plane%d" % c, align_bytes=ALIGN)
             nc.vector.quantize_mx(out=h_words[:].bitcast(FP8X4), scales=h_plane[:], in_=woven[c][:])
-            parts = 2 if c == last else 1
-            blocks = N // P // parts
-            acc[c] = []
-            for part in range(parts):
-                bank = psum.tile([P, blocks, CHUNK], F32, name="acc", tag="pre0" if part else "acc%d" % c)
-                acc[c].append(bank)
+            blocks = N // P // len(banks)
+            sums[c] = []
+            for part, bank in enumerate(banks):
+                acc = psum.tile([P, blocks, CHUNK], F32, name="acc", tag="bank%d" % bank)
+                sums[c].append(acc)
                 for b in range(blocks):
-                    cols = slice(P * (part * blocks + b), P * (part * blocks + b + 1))
+                    n0 = P * (part * blocks + b)
                     nc.tensor.matmul_mx(
-                        out=bank[:, b, :],
-                        lhsT=wb[:, cols].bitcast(FP8X4),
-                        lhsT_scale=wb_plane[:, cols],
+                        out=acc[:, b, :],
+                        lhsT=wb[:, n0 : n0 + P].bitcast(FP8X4),
+                        lhsT_scale=wb_plane[:, n0 : n0 + P],
                         rhs=h_words[:].bitcast(FP8X4),
                         rhs_scale=h_plane[:],
                         start=True,
                         stop=True,
                     )
 
-        def store(c):
-            slots = slice(c * CHUNK, (c + 1) * CHUNK)
-            parts = len(acc[c])
-            blocks = N // P // parts
-            for part in range(parts):
-                res = held.tile([P, blocks, CHUNK], F32, name="res", tag="res%d_%d" % (c, part), align_bytes=64)
-                rows = out_rows[:, part * blocks : (part + 1) * blocks, slots]
-                if c == last and part == 0:
-                    nc.vector.tensor_copy(out=res[:], in_=acc[c][part][:])
-                    nc.sync.dma_start(out=rows, in_=res[:])
-                elif c == last:
-                    nc.scalar.copy(out=res[:], in_=acc[c][part][:])
-                    nc.scalar.dma_start(out=rows, in_=res[:])
-                else:
-                    nc.scalar.copy(out=res[:], in_=acc[c][part][:])
-                    nc.sync.dma_start(out=rows, in_=res[:])
+        out_blocks = out.rearrange("(b p) j -> p b j", p=P)
 
+        def store(c, ways):
+            blocks = N // P // len(ways)
+            for part, (copy, queue) in enumerate(ways):
+                res = sbuf.tile([P, blocks, CHUNK], F32, name="res", tag="res%d_%d" % (c, part), align_bytes=ALIGN)
+                copy(out=res[:], in_=sums[c][part][:])
+                rows = out_blocks[:, part * blocks : (part + 1) * blocks, c * CHUNK : (c + 1) * CHUNK]
+                queue.dma_start(out=rows, in_=res[:])
+
+        first_layer(0, range(PACK))
+        first_layer(1, [PACK])
+        first_layer(2, [PACK + 1])
         for c in range(chunks):
-            add_entries(c)
+            hid = add_entries(c)
             if c > 0:
-                second_layer(c - 1)
-            weave(c)
-            if c > 0:
-                store(c - 1)
-        second_layer(last)
-        store(last)
+                second_layer(c - 1, [c - 1])
+            weave(nc.scalar.copy if c < last else nc.vector.tensor_copy, c, hid)
+            if c == 0:
+                first_layer(last, [PACK + 2])
+            else:
+                store(c - 1, [(nc.scalar.copy, nc.sync)])
+        second_layer(last, [last, PACK + 3])
+        store(last, [(nc.vector.tensor_copy, nc.sync), (nc.scalar.copy, nc.scalar)])

@@ -158,11 +158,11 @@ def tile_moe_expert_hidden_own_entries_kernel(
         for c in range(chunks):
             hid = add_entries(c)
             if c > 0:
-                second_layer(c - 1, [c - 1])
+                second_layer(c - 1, [c - 1, chunks + c - 1])
             weave(nc.scalar.copy if c < last else nc.vector.tensor_copy, c, hid)
             if c == 0:
                 first_layer(last, [PACK + 2])
             else:
-                store(c - 1, [(nc.scalar.copy, nc.sync)])
-        second_layer(last, [last, PACK + 3])
+                store(c - 1, [(nc.scalar.copy, nc.sync)] * 2)
+        second_layer(last, [last, chunks + last])
         store(last, [(nc.vector.tensor_copy, nc.sync), (nc.scalar.copy, nc.scalar)])

from contextlib import ExitStack

import concourse.mybir as mybir

K, T, J, R, N, V = 512, 1024, 512, 512, 512, 512
FLOPS = 2 * K * R * J + 2 * R * N * J

F32 = mybir.dt.float32
BF16 = mybir.dt.bfloat16
I32 = mybir.dt.int32
U32 = mybir.dt.uint32
U16 = mybir.dt.uint16
U8 = mybir.dt.uint8
FP8X4 = mybir.dt.float8_e4m3fn_x4
FP4X4 = mybir.dt.float4_e2m1fn_x4
ADD = mybir.AluOpType.add
RELU = mybir.ActivationFunctionType.Relu

P = 128
PACK = 4
GROUP = 16
QUADRANT = 32
CHUNK = 128
HALF = J // 2
ALIGN = 64


def load_scale_rows(nc, plane, scales):
    for i in range(4):
        nc.sync.dma_start(out=plane[i:P:QUADRANT, :].bitcast(I32), in_=scales[0, i:16:4, :].bitcast(I32))


def by_sheet(raw):
    return raw.rearrange("p (m t) -> p t m", t=PACK)


def tile_moe_expert_hidden_own_entries_kernel(
    tc, xt_words, xt_scales, wa_words, wa_scales, tb, wb_words, wb_scales, offs, offs2, out
):
    nc = tc.nc
    chunks = J // CHUNK
    last = chunks - 1
    with ExitStack() as ctx:
        sbuf = ctx.enter_context(tc.tile_pool(name="sbuf", bufs=1))
        psum = ctx.enter_context(tc.psum_pool(name="psum", bufs=1))

        token_list = sbuf.tile([P, J // GROUP], U16, name="token_list")
        entry_lists = sbuf.tile([P, J // GROUP], U16, name="entry_lists")
        x_words = sbuf.tile([P, T], U32, name="x_words", align_bytes=ALIGN)
        x_plane = sbuf.tile([P, T], U8, name="x_plane", align_bytes=ALIGN)
        wa_raw = sbuf.tile([P, 2 * R], U8, name="wa_raw", align_bytes=ALIGN)
        wa_raw_plane = sbuf.tile([P, R], U8, name="wa_raw_plane", tag="early", align_bytes=ALIGN)
        wa = sbuf.tile([P, 2 * R], U8, name="wa", align_bytes=ALIGN)
        wa_plane = sbuf.tile([P, R], U8, name="wa_plane", align_bytes=ALIGN)
        wb = sbuf.tile([P, N], U32, name="wb", align_bytes=ALIGN)
        wb_plane = sbuf.tile([P, N], U8, name="wb_plane", align_bytes=ALIGN)
        table = [sbuf.tile([P, V], F32, name="table%d" % t, align_bytes=ALIGN) for t in range(PACK)]
        xg_plane = sbuf.tile([P, J], U8, name="xg_plane", align_bytes=ALIGN)

        nc.vector.memset(x_plane[:].bitcast(I32), 0)
        nc.gpsimd.memset(wa_raw_plane[:].bitcast(I32), 0)
        nc.vector.memset(wb_plane[:].bitcast(I32), 0)

        nc.sync.dma_start(token_list[:], offs)
        nc.sync.dma_start(entry_lists[:], offs2)
        nc.sync.dma_start(out=wa_raw[:].bitcast(I32), in_=wa_words[0].bitcast(I32))
        load_scale_rows(nc, x_plane, xt_scales)
        nc.sync.dma_start(out=x_words[:].bitcast(I32), in_=xt_words[0].rearrange("p t r -> p (t r)").bitcast(I32))
        load_scale_rows(nc, wa_raw_plane, wa_scales)
        tb_sheets = tb.rearrange("(p t) v -> p t v", t=PACK)
        for t in range(PACK):
            nc.sync.dma_start(out=table[t][:], in_=tb_sheets[:, t, :])
        nc.sync.dma_start(out=wb[:].bitcast(I32), in_=wb_words[0].rearrange("p n r -> p (n r)").bitcast(I32))
        load_scale_rows(nc, wb_plane, wb_scales)

        nc.vector.tensor_copy(out=wa_plane[:].rearrange("p (t m) -> p t m", t=PACK), in_=by_sheet(wa_raw_plane[:]))
        nc.vector.tensor_copy(
            out=wa[:].bitcast(U16).rearrange("p (t m) -> p t m", t=PACK), in_=by_sheet(wa_raw[:].bitcast(U16))
        )

        nc.vector.tensor_copy(out=xg_plane[:], in_=x_plane[:].indirect(token_list[:]))
        xg_words = []
        for h, tag in enumerate(("xg_first", "early")):
            gathered = sbuf.tile([P, HALF], U32, name="xg_words", tag=tag, align_bytes=ALIGN)
            entries = token_list[:, h * HALF // GROUP : (h + 1) * HALF // GROUP]
            nc.vector.tensor_copy(out=gathered[:], in_=x_words[:].indirect(entries))
            xg_words.append(gathered)

        relu, woven, sums = {}, {}, {}

        def first_layer(c, banks):
            j0 = c * CHUNK
            sheets = PACK // len(banks)
            relu[c] = sbuf.tile([P, PACK, CHUNK], F32, name="relu", tag="relu%d" % c if c else "stage1", align_bytes=ALIGN)
            for part, bank in enumerate(banks):
                pre = psum.tile([P, sheets, CHUNK], F32, name="pre", tag="bank%d" % bank)
                for s in range(sheets):
                    t = part * sheets + s
                    nc.tensor.matmul_mx(
                        out=pre[:, s, :],
                        lhsT=wa[:, 2 * P * t : 2 * P * (t + 1)].bitcast(FP4X4),
                        lhsT_scale=wa_plane[:, P * t : P * (t + 1)],
                        rhs=xg_words[j0 // HALF][:, j0 % HALF : j0 % HALF + CHUNK].bitcast(FP8X4),
                        rhs_scale=xg_plane[:, j0 : j0 + CHUNK],
                        start=True,
                        stop=True,
                    )
                nc.scalar.activation(out=relu[c][:, part * sheets : (part + 1) * sheets, :], in_=pre[:], func=RELU)

        def add_entries(c):
            entries = entry_lists[:, c * CHUNK // GROUP : (c + 1) * CHUNK // GROUP]
            hid = sbuf.tile([P, PACK, CHUNK], F32, name="hid", tag="stage%d" % c, align_bytes=ALIGN)
            for t in range(PACK):
                nc.vector.tensor_tensor(out=hid[:, t, :], in0=table[t][:].indirect(entries), in1=relu[c][:, t, :], op=ADD)
            return hid

        def weave(copy, c, hid):
            woven[c] = sbuf.tile([P, CHUNK * PACK], BF16, name="woven", tag="stage%d" % (c + 2), align_bytes=ALIGN)
            copy(
                out=woven[c][:].rearrange("p (g i t) -> p g t i", i=2, t=PACK),
                in_=hid[:].rearrange("p t (g i) -> p g t i", i=2),
            )

        def second_layer(c, banks):
            h_words = sbuf.tile([P, CHUNK], U32, name="h_words", tag="h_words%d" % c, align_bytes=ALIGN)
            h_plane = sbuf.tile([P, CHUNK], U8, name="h_plane", tag="h_plane%d" % c, align_bytes=ALIGN)
            nc.vector.quantize_mx(out=h_words[:].bitcast(FP8X4), scales=h_plane[:], in_=woven[c][:])
            blocks = N // P // len(banks)
            sums[c] = []
            for part, bank in enumerate(banks):
                acc = psum.tile([P, blocks, CHUNK], F32, name="acc", tag="bank%d" % bank)
                sums[c].append(acc)
                for b in range(blocks):
                    n0 = P * (part * blocks + b)
                    nc.tensor.matmul_mx(
                        out=acc[:, b, :],
                        lhsT=wb[:, n0 : n0 + P].bitcast(FP8X4),
                        lhsT_scale=wb_plane[:, n0 : n0 + P],
                        rhs=h_words[:].bitcast(FP8X4),
                        rhs_scale=h_plane[:],
                        start=True,
                        stop=True,
                    )

        out_blocks = out.rearrange("(b p) j -> p b j", p=P)

        def store(c, ways):
            blocks = N // P // len(ways)
            for part, (copy, queue) in enumerate(ways):
                res = sbuf.tile([P, blocks, CHUNK], F32, name="res", tag="res%d_%d" % (c, part), align_bytes=ALIGN)
                copy(out=res[:], in_=sums[c][part][:])
                rows = out_blocks[:, part * blocks : (part + 1) * blocks, c * CHUNK : (c + 1) * CHUNK]
                queue.dma_start(out=rows, in_=res[:])

        first_layer(0, range(PACK))
        first_layer(1, [PACK])
        first_layer(2, [PACK + 1])
        for c in range(chunks):
            hid = add_entries(c)
            if c > 0:
                second_layer(c - 1, [c - 1, chunks + c - 1])
            weave(nc.scalar.copy if c < last else nc.vector.tensor_copy, c, hid)
            if c == 0:
                first_layer(last, [PACK + 2])
            else:
                store(c - 1, [(nc.scalar.copy, nc.sync)] * 2)
        second_layer(last, [last, chunks + last])
        store(last, [(nc.vector.tensor_copy, nc.sync), (nc.scalar.copy, nc.scalar)])
